import numpy as np
import ml_dtypes


def mxq(x, axis, fmt="e4m3"):
    dtype, down = {"e4m3": (ml_dtypes.float8_e4m3fn, 7), "e5m2": (ml_dtypes.float8_e5m2, 14)}[fmt]
    v = np.moveaxis(np.asarray(x, np.float32).astype(ml_dtypes.bfloat16).astype(np.float64), axis, -1)
    blocks = v.reshape(v.shape[:-1] + (-1, 32))
    amax = np.abs(blocks).max(-1, keepdims=True)
    byte = np.maximum(np.where(amax > 0, np.frexp(amax)[1] - 1 + 127, 0) - down, 1)
    scale = np.exp2(byte - 127.0)
    codes = (blocks / scale).astype(np.float32).astype(dtype).astype(np.float64)
    return np.moveaxis((codes * scale).reshape(v.shape), -1, axis)


WIDE = False


def mx_kscale(k):
    if not WIDE:
        return np.ones(k)
    levels = np.array([10, -10, 5, -5, 0])
    if k % 512:
        return np.exp2(np.random.permutation(np.resize(levels, k // 32))).repeat(32)
    a = np.empty((k // 512, 16))
    for p in range(k // 512):
        a[p, :8] = np.random.permutation(np.resize(levels, 8))
        for g in range(8):
            far = levels[np.abs(levels - a[p, g]) >= 10]
            a[p, g + 8] = far[np.random.randint(len(far))]
    return np.exp2(a.ravel()).repeat(32)


def f64(x):
    return np.asarray(x).astype(np.float64)


def striped(idx):
    return np.tile(np.asarray(idx).reshape(-1, 16).T, (8, 1)).astype(np.uint16)


def unstriped(offs):
    return offs[:16].T.reshape(-1).astype(np.int64)


B, N, C, D, NQ = 1, 512, 2048, 1024, 128
SEG = 16


def eight(codes):
    return np.concatenate([codes[h].reshape(-1, 16).T for h in range(8)]).astype(np.uint16)


def uneight(offs):
    return np.stack([offs[16 * h:16 * h + 16].T.reshape(-1) for h in range(8)]).astype(np.int64)


def setup_inputs():
    n = np.random.standard_normal
    s = mx_kscale(D)[:, None]
    grid = lambda x: np.round(x * 32) / 32
    return {
        "qT": (n((B, D, NQ)) * s / np.sqrt(D)).astype(np.float32),
        "cb": (grid(n((D, C))) / s).astype(np.float32),
        "norm": np.tile(np.random.randint(32, 129, N) / 64.0, (128, 1)).astype(np.float32),
        "offs": eight(np.random.randint(0, C, (8, N))),
        "offs2": eight(np.random.randint(0, C, (8, N))),
    }


def reference(qT, cb, norm, offs, offs2):
    k = []
    for part, offs_ in enumerate((offs, offs2,)):
        codes = uneight(offs_)
        k += [f64(cb)[512 * part + 64 * h:512 * part + 64 * h + 64][:, codes[h]] for h in range(8)]
    k = np.concatenate(k) * f64(norm)[:1]
    a = mxq(f64(qT), 1, "e4m3").transpose(0, 2, 1) @ mxq(k, 0, "e4m3")
    return a.reshape(B, NQ, N // SEG, SEG).max(-1)

@@ -1,0 +1,135 @@
+from contextlib import ExitStack
+
+import concourse.mybir as mybir
+from concourse.masks import make_identity
+
+F32 = mybir.dt.float32
+BF16 = mybir.dt.bfloat16
+U32 = mybir.dt.uint32
+U16 = mybir.dt.uint16
+U8 = mybir.dt.uint8
+FP8X4 = mybir.dt.float8_e4m3fn_x4
+MULT = mybir.AluOpType.mult
+
+P = 128
+PACK = 4
+K_PASS = P * PACK
+D, NQ, N, C = 1024, 128, 512, 2048
+SEG = 16
+PASSES = D // K_PASS
+PIECE = 256
+CHUNKS = ((0, 256), (256, 128), (384, 128))
+
+FLOPS = 2 * NQ * N * D
+
+
+def tile_attend_pq_max16_kernel(tc, qT, cb, norm, offs, offs2, out):
+    nc = tc.nc
+    with ExitStack() as ctx:
+        keep = ctx.enter_context(tc.tile_pool(name="keep", bufs=1))
+        psum = ctx.enter_context(tc.psum_pool(name="psum", bufs=1))
+
+        lists = [keep.tile([P, N // 16], U16, name=f"list{g}") for g in range(PASSES)]
+        planes = [[keep.tile([P, C], F32, name=f"plane{g}_{t}") for t in range(PACK)] for g in range(PASSES)]
+        q_raw = [keep.tile([P, PACK, NQ], F32, name=f"q_raw{g}") for g in range(PASSES)]
+        norm_col = keep.tile([P, PACK], F32, name="norm_col")
+
+        def load_plane(g, t):
+            rows = cb[g * K_PASS:(g + 1) * K_PASS, :].rearrange("(p t) c -> p t c", t=PACK)
+            nc.sync.dma_start(out=planes[g][t][:], in_=rows[:, t, :])
+
+        def load_q(g):
+            nc.sync.dma_start(out=q_raw[g][:], in_=qT[0, g * K_PASS:(g + 1) * K_PASS, :].rearrange("(p t) q -> p t q", t=PACK))
+
+        nc.scalar.dma_start(out=norm_col[:], in_=norm[0:1, :].rearrange("a (p x) -> (a p) x", x=PACK))
+        load_plane(0, 0)
+        nc.sync.dma_start(lists[0][:], offs)
+        load_plane(0, 1)
+        nc.sync.dma_start(lists[1][:], offs2)
+        load_plane(0, 2)
+        load_plane(0, 3)
+        load_q(0)
+        for t in range(PACK):
+            load_plane(1, t)
+        load_q(1)
+
+        ident = keep.tile([P, P], F32, name="ident")
+        make_identity(nc, ident[:])
+        norm_ps = psum.tile([P, PACK, P], F32, name="norm_ps")
+        for j in range(PACK):
+            nc.tensor.transpose(norm_ps[:, j, :], norm_col[:, j:j + 1].to_broadcast([P, P]), ident[:])
+        norm_all = keep.tile([P, N], F32, name="norm_all")
+        nc.vector.tensor_copy(out=norm_all[:].rearrange("p (m j) -> p m j", j=PACK), in_=norm_ps[:].rearrange("p j m -> p m j"))
+
+        q_codes = [keep.tile([P, NQ], U32, align_bytes=64, name=f"q_codes{g}") for g in range(PASSES)]
+        q_scales = [keep.tile([P, NQ], U8, align_bytes=64, name=f"q_scales{g}") for g in range(PASSES)]
+        q_bf = [keep.tile([P, NQ, PACK], BF16, align_bytes=64, name=f"q_bf{g}") for g in range(PASSES)]
+        k_f32 = [keep.tile([P, PACK, N], F32, name=f"k_f32_{g}") for g in range(PASSES)]
+        k_bf = [keep.tile([P, N, PACK], BF16, align_bytes=64, name=f"k_bf{g}") for g in range(PASSES)]
+        k_codes = [keep.tile([P, N], U32, align_bytes=64, name=f"k_codes{g}") for g in range(PASSES)]
+        k_scales = [keep.tile([P, N], U8, align_bytes=64, name=f"k_scales{g}") for g in range(PASSES)]
+        acc = [psum.tile([P, width], F32, name=f"acc{n0}") for n0, width in CHUNKS]
+        best = keep.tile([P, N // SEG], F32, name="best")
+
+        def gather(g, t, n0, width):
+            nc.vector.tensor_tensor(
+                k_f32[g][:, t, n0:n0 + width], planes[g][t][:].indirect(lists[g][:, n0 // 16:(n0 + width) // 16]),
+                norm_all[:, n0:n0 + width], MULT)
+
+        def round_planes(copy, g, t0, t1, n0, width):
+            copy(out=k_bf[g][:, n0:n0 + width, t0:t1], in_=k_f32[g][:, t0:t1, n0:n0 + width].rearrange("p t n -> p n t"))
+
+        def quantise_k(g, n0, width):
+            nc.vector.quantize_mx(out=k_codes[g][:, n0:n0 + width].bitcast(FP8X4), scales=k_scales[g][:, n0:n0 + width],
+                                  in_=k_bf[g][:, n0:n0 + width, :].rearrange("p n t -> p (n t)"))
+
+        def multiply(g, c):
+            n0, width = CHUNKS[c]
+            k_cols = slice(n0, n0 + width)
+            nc.tensor.matmul_mx(out=acc[c][:], lhsT=q_codes[g][:].bitcast(FP8X4), lhsT_scale=q_scales[g][:],
+                                rhs=k_codes[g][:, k_cols].bitcast(FP8X4), rhs_scale=k_scales[g][:, k_cols],
+                                start=(g == 0), stop=(g == PASSES - 1))
+
+        def round_q(copy, g):
+            copy(out=q_bf[g][:], in_=q_raw[g][:].rearrange("p t q -> p q t"))
+
+        def quantise_q(g):
+            nc.vector.quantize_mx(out=q_codes[g][:].bitcast(FP8X4), scales=q_scales[g][:], in_=q_bf[g][:].rearrange("p q t -> p (q t)"))
+
+        def maxima(c):
+            n0, width = CHUNKS[c]
+            nc.vector.tensor_reduce(out=best[:, n0 // SEG:(n0 + width) // SEG], in_=acc[c][:].rearrange("p (j s) -> p j s", s=SEG),
+                                    axis=mybir.AxisListType.X, op=mybir.AluOpType.max)
+
+        for t in range(PACK):
+            for n0 in range(0, N, PIECE):
+                gather(0, t, n0, PIECE)
+        for n0 in range(0, N, PIECE):
+            round_planes(nc.scalar.copy, 0, 0, PACK, n0, PIECE)
+        round_q(nc.scalar.copy, 0)
+        for n0 in range(0, N, PIECE):
+            gather(1, 0, n0, PIECE)
+        quantise_k(0, 0, N)
+        quantise_q(0)
+        for c in range(len(CHUNKS)):
+            multiply(0, c)
+        for t in (1, 2):
+            for n0 in range(0, N, PIECE):
+                gather(1, t, n0, PIECE)
+            if t == 1:
+                for n0 in range(0, N, PIECE):
+                    round_planes(nc.scalar.copy, 1, 0, 2, n0, PIECE)
+        for n0, width in CHUNKS:
+            gather(1, 3, n0, width)
+        round_q(nc.scalar.copy, 1)
+        round_planes(nc.scalar.copy, 1, 2, 4, 0, 256)
+        round_planes(nc.vector.tensor_copy, 1, 2, 4, 256, 128)
+        round_planes(nc.scalar.copy, 1, 2, 4, 384, 128)
+        quantise_q(1)
+        for n0, width in CHUNKS:
+            quantise_k(1, n0, width)
+        for c in range(len(CHUNKS)):
+            multiply(1, c)
+        for c in range(len(CHUNKS)):
+            maxima(c)
+        nc.sync.dma_start(out=out.rearrange("b q j -> (b q) j"), in_=best[:])

@@ -38,20 +38,17 @@ def tile_attend_pq_max16_kernel(tc, qT, cb, norm, offs, offs2, out):
             rows = cb[g * K_PASS:(g + 1) * K_PASS, :].rearrange("(p t) c -> p t c", t=PACK)
             nc.sync.dma_start(out=planes[g][t][:], in_=rows[:, t, :])
 
-        def load_q(g):
-            nc.sync.dma_start(out=q_raw[g][:], in_=qT[0, g * K_PASS:(g + 1) * K_PASS, :].rearrange("(p t) q -> p t q", t=PACK))
+        def load_q(queue, g):
+            queue.dma_start(out=q_raw[g][:], in_=qT[0, g * K_PASS:(g + 1) * K_PASS, :].rearrange("(p t) q -> p t q", t=PACK))
 
-        nc.scalar.dma_start(out=norm_col[:], in_=norm[0:1, :].rearrange("a (p x) -> (a p) x", x=PACK))
-        load_plane(0, 0)
+        load_q(nc.scalar, 0)
         nc.sync.dma_start(lists[0][:], offs)
-        load_plane(0, 1)
         nc.sync.dma_start(lists[1][:], offs2)
-        load_plane(0, 2)
-        load_plane(0, 3)
-        load_q(0)
-        for t in range(PACK):
-            load_plane(1, t)
-        load_q(1)
+        nc.scalar.dma_start(out=norm_col[:], in_=norm[0:1, :].rearrange("a (p x) -> (a p) x", x=PACK))
+        for g in range(PASSES):
+            for t in range(PACK):
+                load_plane(g, t)
+        load_q(nc.sync, 1)
 
         ident = keep.tile([P, P], F32, name="ident")
         make_identity(nc, ident[:])
@@ -102,20 +99,17 @@ def tile_attend_pq_max16_kernel(tc, qT, cb, norm, offs, offs2, out):
                                     axis=mybir.AxisListType.X, op=mybir.AluOpType.max)
 
         for t in range(PACK):
-            for n0 in range(0, N, PIECE):
-                gather(0, t, n0, PIECE)
+            gather(0, t, 0, N)
         for n0 in range(0, N, PIECE):
             round_planes(nc.scalar.copy, 0, 0, PACK, n0, PIECE)
         round_q(nc.scalar.copy, 0)
-        for n0 in range(0, N, PIECE):
-            gather(1, 0, n0, PIECE)
+        gather(1, 0, 0, N)
         quantise_k(0, 0, N)
         quantise_q(0)
         for c in range(len(CHUNKS)):
             multiply(0, c)
         for t in (1, 2):
-            for n0 in range(0, N, PIECE):
-                gather(1, t, n0, PIECE)
+            gather(1, t, 0, N)
             if t == 1:
                 for n0 in range(0, N, PIECE):
                     round_planes(nc.scalar.copy, 1, 0, 2, n0, PIECE)

@@ -18,7 +18,7 @@ D, NQ, N, C = 1024, 128, 512, 2048
 SEG = 16
 PASSES = D // K_PASS
 PIECE = 256
-CHUNKS = ((0, 256), (256, 128), (384, 128))
+CHUNKS = ((0, 128), (128, 128), (256, 128), (384, 128))
 
 FLOPS = 2 * NQ * N * D
 
@@ -88,7 +88,7 @@ def tile_attend_pq_max16_kernel(tc, qT, cb, norm, offs, offs2, out):
                                 start=(g == 0), stop=(g == PASSES - 1))
 
         def round_q(copy, g):
-            copy(out=q_bf[g][:], in_=q_raw[g][:].rearrange("p t q -> p q t"))
+            copy(out=q_bf[g][:].rearrange("p (c i) t -> p c t i", i=PACK), in_=q_raw[g][:].rearrange("p t (c i) -> p c t i", i=PACK))
 
         def quantise_q(g):
             nc.vector.quantize_mx(out=q_codes[g][:].bitcast(FP8X4), scales=q_scales[g][:], in_=q_bf[g][:].rearrange("p q t -> p (q t)"))
@@ -115,10 +115,9 @@ def tile_attend_pq_max16_kernel(tc, qT, cb, norm, offs, offs2, out):
                     round_planes(nc.scalar.copy, 1, 0, 2, n0, PIECE)
         for n0, width in CHUNKS:
             gather(1, 3, n0, width)
-        round_q(nc.scalar.copy, 1)
-        round_planes(nc.scalar.copy, 1, 2, 4, 0, 256)
-        round_planes(nc.vector.tensor_copy, 1, 2, 4, 256, 128)
-        round_planes(nc.scalar.copy, 1, 2, 4, 384, 128)
+        round_q(nc.vector.tensor_copy, 1)
+        for n0, width in CHUNKS:
+            round_planes(nc.scalar.copy, 1, 2, 4, n0, width)
         quantise_q(1)
         for n0, width in CHUNKS:
             quantise_k(1, n0, width)

@@ -42,9 +42,9 @@ def tile_attend_pq_max16_kernel(tc, qT, cb, norm, offs, offs2, out):
             queue.dma_start(out=q_raw[g][:], in_=qT[0, g * K_PASS:(g + 1) * K_PASS, :].rearrange("(p t) q -> p t q", t=PACK))
 
         load_q(nc.scalar, 0)
+        nc.sync.dma_start(out=norm_col[:], in_=norm[0:1, :].rearrange("a (p x) -> (a p) x", x=PACK))
         nc.sync.dma_start(lists[0][:], offs)
         nc.sync.dma_start(lists[1][:], offs2)
-        nc.scalar.dma_start(out=norm_col[:], in_=norm[0:1, :].rearrange("a (p x) -> (a p) x", x=PACK))
         for g in range(PASSES):
             for t in range(PACK):
                 load_plane(g, t)
@@ -76,6 +76,10 @@ def tile_attend_pq_max16_kernel(tc, qT, cb, norm, offs, offs2, out):
         def round_planes(copy, g, t0, t1, n0, width):
             copy(out=k_bf[g][:, n0:n0 + width, t0:t1], in_=k_f32[g][:, t0:t1, n0:n0 + width].rearrange("p t n -> p n t"))
 
+        def round_all_planes(g, n0, width):
+            nc.scalar.copy(out=k_bf[g][:, n0:n0 + width, :].rearrange("p (c i) t -> p c t i", i=PACK),
+                           in_=k_f32[g][:, :, n0:n0 + width].rearrange("p t (c i) -> p c t i", i=PACK))
+
         def quantise_k(g, n0, width):
             nc.vector.quantize_mx(out=k_codes[g][:, n0:n0 + width].bitcast(FP8X4), scales=k_scales[g][:, n0:n0 + width],
                                   in_=k_bf[g][:, n0:n0 + width, :].rearrange("p n t -> p (n t)"))
@@ -101,7 +105,7 @@ def tile_attend_pq_max16_kernel(tc, qT, cb, norm, offs, offs2, out):
         for t in range(PACK):
             gather(0, t, 0, N)
         for n0 in range(0, N, PIECE):
-            round_planes(nc.scalar.copy, 0, 0, PACK, n0, PIECE)
+            round_all_planes(0, n0, PIECE)
         round_q(nc.scalar.copy, 0)
         gather(1, 0, 0, N)
         quantise_k(0, 0, N)

@@ -42,9 +42,9 @@ def tile_attend_pq_max16_kernel(tc, qT, cb, norm, offs, offs2, out):
             queue.dma_start(out=q_raw[g][:], in_=qT[0, g * K_PASS:(g + 1) * K_PASS, :].rearrange("(p t) q -> p t q", t=PACK))
 
         load_q(nc.scalar, 0)
-        nc.sync.dma_start(out=norm_col[:], in_=norm[0:1, :].rearrange("a (p x) -> (a p) x", x=PACK))
         nc.sync.dma_start(lists[0][:], offs)
         nc.sync.dma_start(lists[1][:], offs2)
+        nc.scalar.dma_start(out=norm_col[:], in_=norm[0:1, :].rearrange("a (p x) -> (a p) x", x=PACK))
         for g in range(PASSES):
             for t in range(PACK):
                 load_plane(g, t)

@@ -42,12 +42,13 @@ def tile_attend_pq_max16_kernel(tc, qT, cb, norm, offs, offs2, out):
             queue.dma_start(out=q_raw[g][:], in_=qT[0, g * K_PASS:(g + 1) * K_PASS, :].rearrange("(p t) q -> p t q", t=PACK))
 
         load_q(nc.scalar, 0)
-        nc.sync.dma_start(lists[0][:], offs)
-        nc.sync.dma_start(lists[1][:], offs2)
         nc.scalar.dma_start(out=norm_col[:], in_=norm[0:1, :].rearrange("a (p x) -> (a p) x", x=PACK))
-        for g in range(PASSES):
-            for t in range(PACK):
-                load_plane(g, t)
+        load_plane(0, 0)
+        nc.sync.dma_start(lists[0][:], offs)
+        load_plane(0, 1)
+        nc.sync.dma_start(lists[1][:], offs2)
+        for plane in range(2, PASSES * PACK):
+            load_plane(*divmod(plane, PACK))
         load_q(nc.sync, 1)
 
         ident = keep.tile([P, P], F32, name="ident")

@@ -18,7 +18,8 @@ D, NQ, N, C = 1024, 128, 512, 2048
 SEG = 16
 PASSES = D // K_PASS
 PIECE = 256
-CHUNKS = ((0, 128), (128, 128), (256, 128), (384, 128))
+CHUNKS = ((0, 128), (128, 256), (384, 128))
+STEP = 128
 
 FLOPS = 2 * NQ * N * D
 
@@ -118,11 +119,11 @@ def tile_attend_pq_max16_kernel(tc, qT, cb, norm, offs, offs2, out):
             if t == 1:
                 for n0 in range(0, N, PIECE):
                     round_planes(nc.scalar.copy, 1, 0, 2, n0, PIECE)
-        for n0, width in CHUNKS:
-            gather(1, 3, n0, width)
+        for n0 in range(0, N, STEP):
+            gather(1, 3, n0, STEP)
         round_q(nc.vector.tensor_copy, 1)
-        for n0, width in CHUNKS:
-            round_planes(nc.scalar.copy, 1, 2, 4, n0, width)
+        for n0 in range(0, N, STEP):
+            round_planes(nc.scalar.copy, 1, 2, 4, n0, STEP)
         quantise_q(1)
         for n0, width in CHUNKS:
             quantise_k(1, n0, width)
@@ -130,4 +131,4 @@ def tile_attend_pq_max16_kernel(tc, qT, cb, norm, offs, offs2, out):
             multiply(1, c)
         for c in range(len(CHUNKS)):
             maxima(c)
-        nc.sync.dma_start(out=out.rearrange("b q j -> (b q) j"), in_=best[:])
+        nc.scalar.dma_start(out=out.rearrange("b q j -> (b q) j"), in_=best[:])

@@ -18,7 +18,7 @@ D, NQ, N, C = 1024, 128, 512, 2048
 SEG = 16
 PASSES = D // K_PASS
 PIECE = 256
-CHUNKS = ((0, 128), (128, 256), (384, 128))
+CHUNKS = ((0, 128), (128, 128), (256, 128), (384, 128))
 STEP = 128
 
 FLOPS = 2 * NQ * N * D
@@ -32,24 +32,23 @@ def tile_attend_pq_max16_kernel(tc, qT, cb, norm, offs, offs2, out):
 
         lists = [keep.tile([P, N // 16], U16, name=f"list{g}") for g in range(PASSES)]
         planes = [[keep.tile([P, C], F32, name=f"plane{g}_{t}") for t in range(PACK)] for g in range(PASSES)]
-        q_raw = [keep.tile([P, PACK, NQ], F32, name=f"q_raw{g}") for g in range(PASSES)]
+        q_raw = [keep.tile([P, PACK, NQ], F32, align_bytes=64, name=f"q_raw{g}", tag=f"q_raw{g}") for g in range(PASSES)]
         norm_col = keep.tile([P, PACK], F32, name="norm_col")
 
-        def load_plane(g, t):
+        def load_plane(queue, g, t):
             rows = cb[g * K_PASS:(g + 1) * K_PASS, :].rearrange("(p t) c -> p t c", t=PACK)
-            nc.sync.dma_start(out=planes[g][t][:], in_=rows[:, t, :])
+            queue.dma_start(out=planes[g][t][:], in_=rows[:, t, :])
 
         def load_q(queue, g):
             queue.dma_start(out=q_raw[g][:], in_=qT[0, g * K_PASS:(g + 1) * K_PASS, :].rearrange("(p t) q -> p t q", t=PACK))
 
-        load_q(nc.scalar, 0)
+        load_plane(nc.scalar, 0, 0)
         nc.scalar.dma_start(out=norm_col[:], in_=norm[0:1, :].rearrange("a (p x) -> (a p) x", x=PACK))
-        load_plane(0, 0)
         nc.sync.dma_start(lists[0][:], offs)
-        load_plane(0, 1)
         nc.sync.dma_start(lists[1][:], offs2)
-        for plane in range(2, PASSES * PACK):
-            load_plane(*divmod(plane, PACK))
+        for plane in range(1, PASSES * PACK):
+            load_plane(nc.sync, *divmod(plane, PACK))
+        load_q(nc.sync, 0)
         load_q(nc.sync, 1)
 
         ident = keep.tile([P, P], F32, name="ident")
@@ -108,27 +107,32 @@ def tile_attend_pq_max16_kernel(tc, qT, cb, norm, offs, offs2, out):
             gather(0, t, 0, N)
         for n0 in range(0, N, PIECE):
             round_all_planes(0, n0, PIECE)
-        round_q(nc.scalar.copy, 0)
         gather(1, 0, 0, N)
         quantise_k(0, 0, N)
-        quantise_q(0)
-        for c in range(len(CHUNKS)):
-            multiply(0, c)
         for t in (1, 2):
             gather(1, t, 0, N)
             if t == 1:
-                for n0 in range(0, N, PIECE):
-                    round_planes(nc.scalar.copy, 1, 0, 2, n0, PIECE)
-        for n0 in range(0, N, STEP):
-            gather(1, 3, n0, STEP)
-        round_q(nc.vector.tensor_copy, 1)
-        for n0 in range(0, N, STEP):
+                for n0, width in ((128, 128), (256, 256)):
+                    round_planes(nc.scalar.copy, 1, 0, 2, n0, width)
+        for n0, width in ((0, 128), (128, 256), (384, 128)):
+            gather(1, 3, n0, width)
+        round_q(nc.scalar.copy, 0)
+        for n0 in (128, 256, 384):
             round_planes(nc.scalar.copy, 1, 2, 4, n0, STEP)
+        round_q(nc.vector.tensor_copy, 1)
+        quantise_q(0)
         quantise_q(1)
-        for n0, width in CHUNKS:
-            quantise_k(1, n0, width)
-        for c in range(len(CHUNKS)):
-            multiply(1, c)
-        for c in range(len(CHUNKS)):
+        own_bf = keep.tile([P, STEP, PACK], BF16, align_bytes=64, name="own_bf", tag="q_raw1")
+        nc.vector.tensor_copy(out=own_bf[:].rearrange("p (c i) t -> p c t i", i=PACK),
+                              in_=k_f32[1][:, :, 0:STEP].rearrange("p t (c i) -> p c t i", i=PACK))
+        quantise_k(1, 128, STEP)
+        quantise_k(1, 256, STEP)
+        nc.vector.quantize_mx(out=k_codes[1][:, 0:STEP].bitcast(FP8X4), scales=k_scales[1][:, 0:STEP],
+                              in_=own_bf[:].rearrange("p n t -> p (n t)"))
+        quantise_k(1, 384, STEP)
+        for g in range(PASSES):
+            for c in (1, 2, 0, 3):
+                multiply(g, c)
+        for c in (1, 2, 0, 3):
             maxima(c)
         nc.scalar.dma_start(out=out.rearrange("b q j -> (b q) j"), in_=best[:])

@@ -43,7 +43,7 @@ def tile_attend_pq_max16_kernel(tc, qT, cb, norm, offs, offs2, out):
             queue.dma_start(out=q_raw[g][:], in_=qT[0, g * K_PASS:(g + 1) * K_PASS, :].rearrange("(p t) q -> p t q", t=PACK))
 
         load_plane(nc.scalar, 0, 0)
-        nc.scalar.dma_start(out=norm_col[:], in_=norm[0:1, :].rearrange("a (p x) -> (a p) x", x=PACK))
+        nc.sync.dma_start(out=norm_col[:], in_=norm[0:1, :].rearrange("a (p x) -> (a p) x", x=PACK))
         nc.sync.dma_start(lists[0][:], offs)
         nc.sync.dma_start(lists[1][:], offs2)
         for plane in range(1, PASSES * PACK):
@@ -57,7 +57,7 @@ def tile_attend_pq_max16_kernel(tc, qT, cb, norm, offs, offs2, out):
         for j in range(PACK):
             nc.tensor.transpose(norm_ps[:, j, :], norm_col[:, j:j + 1].to_broadcast([P, P]), ident[:])
         norm_all = keep.tile([P, N], F32, name="norm_all")
-        nc.vector.tensor_copy(out=norm_all[:].rearrange("p (m j) -> p m j", j=PACK), in_=norm_ps[:].rearrange("p j m -> p m j"))
+        nc.scalar.copy(out=norm_all[:].rearrange("p (m j) -> p m j", j=PACK), in_=norm_ps[:].rearrange("p j m -> p m j"))
 
         q_codes = [keep.tile([P, NQ], U32, align_bytes=64, name=f"q_codes{g}") for g in range(PASSES)]
         q_scales = [keep.tile([P, NQ], U8, align_bytes=64, name=f"q_scales{g}") for g in range(PASSES)]

@@ -35,17 +35,18 @@ def tile_attend_pq_max16_kernel(tc, qT, cb, norm, offs, offs2, out):
         q_raw = [keep.tile([P, PACK, NQ], F32, align_bytes=64, name=f"q_raw{g}", tag=f"q_raw{g}") for g in range(PASSES)]
         norm_col = keep.tile([P, PACK], F32, name="norm_col")
 
-        def load_plane(queue, g, t):
+        def load_plane(queue, g, t, c0=0, c1=C):
             rows = cb[g * K_PASS:(g + 1) * K_PASS, :].rearrange("(p t) c -> p t c", t=PACK)
-            queue.dma_start(out=planes[g][t][:], in_=rows[:, t, :])
+            queue.dma_start(out=planes[g][t][:, c0:c1], in_=rows[:, t, c0:c1])
 
         def load_q(queue, g):
             queue.dma_start(out=q_raw[g][:], in_=qT[0, g * K_PASS:(g + 1) * K_PASS, :].rearrange("(p t) q -> p t q", t=PACK))
 
-        load_plane(nc.scalar, 0, 0)
+        load_plane(nc.scalar, 0, 0, 0, C // 2)
         nc.sync.dma_start(out=norm_col[:], in_=norm[0:1, :].rearrange("a (p x) -> (a p) x", x=PACK))
         nc.sync.dma_start(lists[0][:], offs)
         nc.sync.dma_start(lists[1][:], offs2)
+        load_plane(nc.sync, 0, 0, C // 2, C)
         for plane in range(1, PASSES * PACK):
             load_plane(nc.sync, *divmod(plane, PACK))
         load_q(nc.sync, 0)

@@ -113,27 +113,29 @@ def tile_attend_pq_max16_kernel(tc, qT, cb, norm, offs, offs2, out):
         for t in (1, 2):
             gather(1, t, 0, N)
             if t == 1:
-                for n0, width in ((128, 128), (256, 256)):
+                for n0, width in ((384, 128), (0, 256)):
                     round_planes(nc.scalar.copy, 1, 0, 2, n0, width)
-        for n0, width in ((0, 128), (128, 256), (384, 128)):
+        for n0, width in ((256, 128), (0, 256), (384, 128)):
             gather(1, 3, n0, width)
         round_q(nc.scalar.copy, 0)
-        for n0 in (128, 256, 384):
+        for n0 in (0, 128, 384):
             round_planes(nc.scalar.copy, 1, 2, 4, n0, STEP)
         round_q(nc.vector.tensor_copy, 1)
         quantise_q(0)
         quantise_q(1)
         own_bf = keep.tile([P, STEP, PACK], BF16, align_bytes=64, name="own_bf", tag="q_raw1")
         nc.vector.tensor_copy(out=own_bf[:].rearrange("p (c i) t -> p c t i", i=PACK),
-                              in_=k_f32[1][:, :, 0:STEP].rearrange("p t (c i) -> p c t i", i=PACK))
+                              in_=k_f32[1][:, :, 256:384].rearrange("p t (c i) -> p c t i", i=PACK))
+        quantise_k(1, 0, STEP)
         quantise_k(1, 128, STEP)
-        quantise_k(1, 256, STEP)
-        nc.vector.quantize_mx(out=k_codes[1][:, 0:STEP].bitcast(FP8X4), scales=k_scales[1][:, 0:STEP],
+        nc.vector.quantize_mx(out=k_codes[1][:, 256:384].bitcast(FP8X4), scales=k_scales[1][:, 256:384],
                               in_=own_bf[:].rearrange("p n t -> p (n t)"))
         quantise_k(1, 384, STEP)
         for g in range(PASSES):
-            for c in (1, 2, 0, 3):
+            for c in range(4):
                 multiply(g, c)
-        for c in (1, 2, 0, 3):
+        for c in range(4):
             maxima(c)
-        nc.scalar.dma_start(out=out.rearrange("b q j -> (b q) j"), in_=best[:])
+        rows = out.rearrange("b q j -> (b q) j")
+        nc.sync.dma_start(out=rows[:, 0:16], in_=best[:, 0:16])
+        nc.scalar.dma_start(out=rows[:, 16:32], in_=best[:, 16:32])

@@ -62,7 +62,7 @@ def tile_attend_pq_max16_kernel(tc, qT, cb, norm, offs, offs2, out):
 
         q_codes = [keep.tile([P, NQ], U32, align_bytes=64, name=f"q_codes{g}") for g in range(PASSES)]
         q_scales = [keep.tile([P, NQ], U8, align_bytes=64, name=f"q_scales{g}") for g in range(PASSES)]
-        q_bf = [keep.tile([P, NQ, PACK], BF16, align_bytes=64, name=f"q_bf{g}") for g in range(PASSES)]
+        q_bf = [keep.tile([P, NQ, PACK], BF16, align_bytes=64, name="q_bf0")]
         k_f32 = [keep.tile([P, PACK, N], F32, name=f"k_f32_{g}") for g in range(PASSES)]
         k_bf = [keep.tile([P, N, PACK], BF16, align_bytes=64, name=f"k_bf{g}") for g in range(PASSES)]
         k_codes = [keep.tile([P, N], U32, align_bytes=64, name=f"k_codes{g}") for g in range(PASSES)]
@@ -89,8 +89,9 @@ def tile_attend_pq_max16_kernel(tc, qT, cb, norm, offs, offs2, out):
         def multiply(g, c):
             n0, width = CHUNKS[c]
             k_cols = slice(n0, n0 + width)
+            codes = own_codes[:] if (g, c) == (1, 2) else k_codes[g][:, k_cols]
             nc.tensor.matmul_mx(out=acc[c][:], lhsT=q_codes[g][:].bitcast(FP8X4), lhsT_scale=q_scales[g][:],
-                                rhs=k_codes[g][:, k_cols].bitcast(FP8X4), rhs_scale=k_scales[g][:, k_cols],
+                                rhs=codes.bitcast(FP8X4), rhs_scale=k_scales[g][:, k_cols],
                                 start=(g == 0), stop=(g == PASSES - 1))
 
         def round_q(copy, g):
@@ -113,23 +114,23 @@ def tile_attend_pq_max16_kernel(tc, qT, cb, norm, offs, offs2, out):
         for t in (1, 2):
             gather(1, t, 0, N)
             if t == 1:
-                for n0, width in ((384, 128), (0, 256)):
+                for n0, width in ((256, 256), (0, 256)):
                     round_planes(nc.scalar.copy, 1, 0, 2, n0, width)
         for n0, width in ((256, 128), (0, 256), (384, 128)):
             gather(1, 3, n0, width)
         round_q(nc.scalar.copy, 0)
         for n0 in (0, 128, 384):
             round_planes(nc.scalar.copy, 1, 2, 4, n0, STEP)
-        round_q(nc.vector.tensor_copy, 1)
+        round_planes(nc.vector.tensor_copy, 1, 2, 4, 256, STEP)
         quantise_q(0)
-        quantise_q(1)
-        own_bf = keep.tile([P, STEP, PACK], BF16, align_bytes=64, name="own_bf", tag="q_raw1")
-        nc.vector.tensor_copy(out=own_bf[:].rearrange("p (c i) t -> p c t i", i=PACK),
-                              in_=k_f32[1][:, :, 256:384].rearrange("p t (c i) -> p c t i", i=PACK))
+        q_bf.append(keep.tile([P, NQ, PACK], BF16, align_bytes=64, name="q_bf1", tag="q_raw0"))
+        round_q(nc.vector.tensor_copy, 1)
         quantise_k(1, 0, STEP)
+        quantise_q(1)
+        own_codes = keep.tile([P, STEP], U32, align_bytes=64, name="own_codes", tag="q_raw1")
         quantise_k(1, 128, STEP)
-        nc.vector.quantize_mx(out=k_codes[1][:, 256:384].bitcast(FP8X4), scales=k_scales[1][:, 256:384],
-                              in_=own_bf[:].rearrange("p n t -> p (n t)"))
+        nc.vector.quantize_mx(out=own_codes[:].bitcast(FP8X4), scales=k_scales[1][:, 256:384],
+                              in_=k_bf[1][:, 256:384, :].rearrange("p n t -> p (n t)"))
         quantise_k(1, 384, STEP)
         for g in range(PASSES):
             for c in range(4):

@@ -119,9 +119,9 @@ def tile_attend_pq_max16_kernel(tc, qT, cb, norm, offs, offs2, out):
         for n0, width in ((256, 128), (0, 256), (384, 128)):
             gather(1, 3, n0, width)
         round_q(nc.scalar.copy, 0)
-        for n0 in (0, 128, 384):
-            round_planes(nc.scalar.copy, 1, 2, 4, n0, STEP)
-        round_planes(nc.vector.tensor_copy, 1, 2, 4, 256, STEP)
+        for n0, width in ((0, 128), (128, 64), (384, 128)):
+            round_planes(nc.scalar.copy, 1, 2, 4, n0, width)
+        round_planes(nc.vector.tensor_copy, 1, 2, 4, 192, 192)
         quantise_q(0)
         q_bf.append(keep.tile([P, NQ, PACK], BF16, align_bytes=64, name="q_bf1", tag="q_raw0"))
         round_q(nc.vector.tensor_copy, 1)

@@ -17,7 +17,6 @@ K_PASS = P * PACK
 D, NQ, N, C = 1024, 128, 512, 2048
 SEG = 16
 PASSES = D // K_PASS
-PIECE = 256
 CHUNKS = ((0, 128), (128, 128), (256, 128), (384, 128))
 STEP = 128
 
@@ -78,10 +77,6 @@ def tile_attend_pq_max16_kernel(tc, qT, cb, norm, offs, offs2, out):
         def round_planes(copy, g, t0, t1, n0, width):
             copy(out=k_bf[g][:, n0:n0 + width, t0:t1], in_=k_f32[g][:, t0:t1, n0:n0 + width].rearrange("p t n -> p n t"))
 
-        def round_all_planes(g, n0, width):
-            nc.scalar.copy(out=k_bf[g][:, n0:n0 + width, :].rearrange("p (c i) t -> p c t i", i=PACK),
-                           in_=k_f32[g][:, :, n0:n0 + width].rearrange("p t (c i) -> p c t i", i=PACK))
-
         def quantise_k(g, n0, width):
             nc.vector.quantize_mx(out=k_codes[g][:, n0:n0 + width].bitcast(FP8X4), scales=k_scales[g][:, n0:n0 + width],
                                   in_=k_bf[g][:, n0:n0 + width, :].rearrange("p n t -> p (n t)"))
@@ -107,8 +102,8 @@ def tile_attend_pq_max16_kernel(tc, qT, cb, norm, offs, offs2, out):
 
         for t in range(PACK):
             gather(0, t, 0, N)
-        for n0 in range(0, N, PIECE):
-            round_all_planes(0, n0, PIECE)
+            if t % 2:
+                round_planes(nc.scalar.copy, 0, t - 1, t + 1, 0, N)
         gather(1, 0, 0, N)
         quantise_k(0, 0, N)
         for t in (1, 2):

@@ -84,7 +84,7 @@ def tile_attend_pq_max16_kernel(tc, qT, cb, norm, offs, offs2, out):
         def multiply(g, c):
             n0, width = CHUNKS[c]
             k_cols = slice(n0, n0 + width)
-            codes = own_codes[:] if (g, c) == (1, 2) else k_codes[g][:, k_cols]
+            codes = k_codes[g][:, k_cols]
             nc.tensor.matmul_mx(out=acc[c][:], lhsT=q_codes[g][:].bitcast(FP8X4), lhsT_scale=q_scales[g][:],
                                 rhs=codes.bitcast(FP8X4), rhs_scale=k_scales[g][:, k_cols],
                                 start=(g == 0), stop=(g == PASSES - 1))
@@ -111,21 +111,19 @@ def tile_attend_pq_max16_kernel(tc, qT, cb, norm, offs, offs2, out):
             if t == 1:
                 for n0, width in ((256, 256), (0, 256)):
                     round_planes(nc.scalar.copy, 1, 0, 2, n0, width)
-        for n0, width in ((256, 128), (0, 256), (384, 128)):
+        for n0, width in ((0, 384), (384, 128)):
             gather(1, 3, n0, width)
         round_q(nc.scalar.copy, 0)
-        for n0, width in ((0, 128), (128, 64), (384, 128)):
-            round_planes(nc.scalar.copy, 1, 2, 4, n0, width)
-        round_planes(nc.vector.tensor_copy, 1, 2, 4, 192, 192)
+        round_planes(nc.scalar.copy, 1, 2, 4, 0, 128)
+        round_planes(nc.scalar.copy, 1, 2, 4, 288, 96)
+        round_planes(nc.scalar.copy, 1, 2, 4, 384, 128)
+        round_planes(nc.vector.tensor_copy, 1, 2, 4, 128, 160)
         quantise_q(0)
         q_bf.append(keep.tile([P, NQ, PACK], BF16, align_bytes=64, name="q_bf1", tag="q_raw0"))
         round_q(nc.vector.tensor_copy, 1)
-        quantise_k(1, 0, STEP)
+        quantise_k(1, 0, 256)
         quantise_q(1)
-        own_codes = keep.tile([P, STEP], U32, align_bytes=64, name="own_codes", tag="q_raw1")
-        quantise_k(1, 128, STEP)
-        nc.vector.quantize_mx(out=own_codes[:].bitcast(FP8X4), scales=k_scales[1][:, 256:384],
-                              in_=k_bf[1][:, 256:384, :].rearrange("p n t -> p (n t)"))
+        quantise_k(1, 256, STEP)
         quantise_k(1, 384, STEP)
         for g in range(PASSES):
             for c in range(4):

@@ -41,11 +41,11 @@ def tile_attend_pq_max16_kernel(tc, qT, cb, norm, offs, offs2, out):
         def load_q(queue, g):
             queue.dma_start(out=q_raw[g][:], in_=qT[0, g * K_PASS:(g + 1) * K_PASS, :].rearrange("(p t) q -> p t q", t=PACK))
 
-        load_plane(nc.scalar, 0, 0, 0, C // 2)
+        load_plane(nc.sync, 0, 0, 0, C // 4)
+        load_plane(nc.scalar, 0, 0, C // 4, C)
         nc.sync.dma_start(out=norm_col[:], in_=norm[0:1, :].rearrange("a (p x) -> (a p) x", x=PACK))
         nc.sync.dma_start(lists[0][:], offs)
         nc.sync.dma_start(lists[1][:], offs2)
-        load_plane(nc.sync, 0, 0, C // 2, C)
         for plane in range(1, PASSES * PACK):
             load_plane(nc.sync, *divmod(plane, PACK))
         load_q(nc.sync, 0)
@@ -131,5 +131,5 @@ def tile_attend_pq_max16_kernel(tc, qT, cb, norm, offs, offs2, out):
         for c in range(4):
             maxima(c)
         rows = out.rearrange("b q j -> (b q) j")
-        nc.sync.dma_start(out=rows[:, 0:16], in_=best[:, 0:16])
-        nc.scalar.dma_start(out=rows[:, 16:32], in_=best[:, 16:32])
+        nc.scalar.dma_start(out=rows[:, 0:16], in_=best[:, 0:16])
+        nc.sync.dma_start(out=rows[:, 16:32], in_=best[:, 16:32])

@@ -19,6 +19,7 @@ SEG = 16
 PASSES = D // K_PASS
 CHUNKS = ((0, 128), (128, 128), (256, 128), (384, 128))
 STEP = 128
+HALF = P // 2
 
 FLOPS = 2 * NQ * N * D
 
@@ -32,7 +33,7 @@ def tile_attend_pq_max16_kernel(tc, qT, cb, norm, offs, offs2, out):
         lists = [keep.tile([P, N // 16], U16, name=f"list{g}") for g in range(PASSES)]
         planes = [[keep.tile([P, C], F32, name=f"plane{g}_{t}") for t in range(PACK)] for g in range(PASSES)]
         q_raw = [keep.tile([P, PACK, NQ], F32, align_bytes=64, name=f"q_raw{g}", tag=f"q_raw{g}") for g in range(PASSES)]
-        norm_col = keep.tile([P, PACK], F32, name="norm_col")
+        norm_col = keep.tile([P, N // HALF], F32, name="norm_col")
 
         def load_plane(queue, g, t, c0=0, c1=C):
             rows = cb[g * K_PASS:(g + 1) * K_PASS, :].rearrange("(p t) c -> p t c", t=PACK)
@@ -43,7 +44,7 @@ def tile_attend_pq_max16_kernel(tc, qT, cb, norm, offs, offs2, out):
 
         load_plane(nc.sync, 0, 0, 0, C // 4)
         load_plane(nc.scalar, 0, 0, C // 4, C)
-        nc.sync.dma_start(out=norm_col[:], in_=norm[0:1, :].rearrange("a (p x) -> (a p) x", x=PACK))
+        nc.sync.dma_start(out=norm_col[0:HALF, :], in_=norm[0:1, :].rearrange("a (p x) -> (a p) x", p=HALF))
         nc.sync.dma_start(lists[0][:], offs)
         nc.sync.dma_start(lists[1][:], offs2)
         for plane in range(1, PASSES * PACK):
@@ -53,11 +54,15 @@ def tile_attend_pq_max16_kernel(tc, qT, cb, norm, offs, offs2, out):
 
         ident = keep.tile([P, P], F32, name="ident")
         make_identity(nc, ident[:])
-        norm_ps = psum.tile([P, PACK, P], F32, name="norm_ps")
-        for j in range(PACK):
-            nc.tensor.transpose(norm_ps[:, j, :], norm_col[:, j:j + 1].to_broadcast([P, P]), ident[:])
+        nc.vector.memset(norm_col[HALF:P, :], 0.0)
         norm_all = keep.tile([P, N], F32, name="norm_all")
-        nc.scalar.copy(out=norm_all[:].rearrange("p (m j) -> p m j", j=PACK), in_=norm_ps[:].rearrange("p j m -> p m j"))
+        for bank in range(2):
+            norm_ps = psum.tile([P, PACK, P], F32, name=f"norm_ps{bank}")
+            for j in range(PACK):
+                col = bank * PACK + j
+                nc.tensor.transpose(norm_ps[:, j, :], norm_col[:, col:col + 1].to_broadcast([P, P]), ident[:])
+            nc.scalar.copy(out=norm_all[:].rearrange("p (m b j) -> p m b j", b=2, j=PACK)[:, :, bank, :],
+                           in_=norm_ps[:, :, 0:HALF].rearrange("p j m -> p m j"))
 
         q_codes = [keep.tile([P, NQ], U32, align_bytes=64, name=f"q_codes{g}") for g in range(PASSES)]
         q_scales = [keep.tile([P, NQ], U8, align_bytes=64, name=f"q_scales{g}") for g in range(PASSES)]

from contextlib import ExitStack

import concourse.mybir as mybir
from concourse.masks import make_identity

F32 = mybir.dt.float32
BF16 = mybir.dt.bfloat16
U32 = mybir.dt.uint32
U16 = mybir.dt.uint16
U8 = mybir.dt.uint8
FP8X4 = mybir.dt.float8_e4m3fn_x4
MULT = mybir.AluOpType.mult

P = 128
PACK = 4
K_PASS = P * PACK
D, NQ, N, C = 1024, 128, 512, 2048
SEG = 16
PASSES = D // K_PASS
CHUNKS = ((0, 128), (128, 128), (256, 128), (384, 128))
STEP = 128
HALF = P // 2

FLOPS = 2 * NQ * N * D


def tile_attend_pq_max16_kernel(tc, qT, cb, norm, offs, offs2, out):
    nc = tc.nc
    with ExitStack() as ctx:
        keep = ctx.enter_context(tc.tile_pool(name="keep", bufs=1))
        psum = ctx.enter_context(tc.psum_pool(name="psum", bufs=1))

        lists = [keep.tile([P, N // 16], U16, name=f"list{g}") for g in range(PASSES)]
        planes = [[keep.tile([P, C], F32, name=f"plane{g}_{t}") for t in range(PACK)] for g in range(PASSES)]
        q_raw = [keep.tile([P, PACK, NQ], F32, align_bytes=64, name=f"q_raw{g}", tag=f"q_raw{g}") for g in range(PASSES)]
        norm_col = keep.tile([P, N // HALF], F32, name="norm_col")

        def load_plane(queue, g, t, c0=0, c1=C):
            rows = cb[g * K_PASS:(g + 1) * K_PASS, :].rearrange("(p t) c -> p t c", t=PACK)
            queue.dma_start(out=planes[g][t][:, c0:c1], in_=rows[:, t, c0:c1])

        def load_q(queue, g):
            queue.dma_start(out=q_raw[g][:], in_=qT[0, g * K_PASS:(g + 1) * K_PASS, :].rearrange("(p t) q -> p t q", t=PACK))

        load_plane(nc.sync, 0, 0, 0, C // 4)
        load_plane(nc.scalar, 0, 0, C // 4, C)
        nc.sync.dma_start(out=norm_col[0:HALF, :], in_=norm[0:1, :].rearrange("a (p x) -> (a p) x", p=HALF))
        nc.sync.dma_start(lists[0][:], offs)
        nc.sync.dma_start(lists[1][:], offs2)
        for plane in range(1, PASSES * PACK):
            load_plane(nc.sync, *divmod(plane, PACK))
        load_q(nc.sync, 0)
        load_q(nc.sync, 1)

        ident = keep.tile([P, P], F32, name="ident")
        make_identity(nc, ident[:])
        nc.vector.memset(norm_col[HALF:P, :], 0.0)
        norm_all = keep.tile([P, N], F32, name="norm_all")
        for bank in range(2):
            norm_ps = psum.tile([P, PACK, P], F32, name=f"norm_ps{bank}")
            for j in range(PACK):
                col = bank * PACK + j
                nc.tensor.transpose(norm_ps[:, j, :], norm_col[:, col:col + 1].to_broadcast([P, P]), ident[:])
            nc.scalar.copy(out=norm_all[:].rearrange("p (m b j) -> p m b j", b=2, j=PACK)[:, :, bank, :],
                           in_=norm_ps[:, :, 0:HALF].rearrange("p j m -> p m j"))

        q_codes = [keep.tile([P, NQ], U32, align_bytes=64, name=f"q_codes{g}") for g in range(PASSES)]
        q_scales = [keep.tile([P, NQ], U8, align_bytes=64, name=f"q_scales{g}") for g in range(PASSES)]
        q_bf = [keep.tile([P, NQ, PACK], BF16, align_bytes=64, name="q_bf0")]
        k_f32 = [keep.tile([P, PACK, N], F32, name=f"k_f32_{g}") for g in range(PASSES)]
        k_bf = [keep.tile([P, N, PACK], BF16, align_bytes=64, name=f"k_bf{g}") for g in range(PASSES)]
        k_codes = [keep.tile([P, N], U32, align_bytes=64, name=f"k_codes{g}") for g in range(PASSES)]
        k_scales = [keep.tile([P, N], U8, align_bytes=64, name=f"k_scales{g}") for g in range(PASSES)]
        acc = [psum.tile([P, width], F32, name=f"acc{n0}") for n0, width in CHUNKS]
        best = keep.tile([P, N // SEG], F32, name="best")

        def gather(g, t, n0, width):
            nc.vector.tensor_tensor(
                k_f32[g][:, t, n0:n0 + width], planes[g][t][:].indirect(lists[g][:, n0 // 16:(n0 + width) // 16]),
                norm_all[:, n0:n0 + width], MULT)

        def round_planes(copy, g, t0, t1, n0, width):
            copy(out=k_bf[g][:, n0:n0 + width, t0:t1], in_=k_f32[g][:, t0:t1, n0:n0 + width].rearrange("p t n -> p n t"))

        def quantise_k(g, n0, width):
            nc.vector.quantize_mx(out=k_codes[g][:, n0:n0 + width].bitcast(FP8X4), scales=k_scales[g][:, n0:n0 + width],
                                  in_=k_bf[g][:, n0:n0 + width, :].rearrange("p n t -> p (n t)"))

        def multiply(g, c):
            n0, width = CHUNKS[c]
            k_cols = slice(n0, n0 + width)
            codes = k_codes[g][:, k_cols]
            nc.tensor.matmul_mx(out=acc[c][:], lhsT=q_codes[g][:].bitcast(FP8X4), lhsT_scale=q_scales[g][:],
                                rhs=codes.bitcast(FP8X4), rhs_scale=k_scales[g][:, k_cols],
                                start=(g == 0), stop=(g == PASSES - 1))

        def round_q(copy, g):
            copy(out=q_bf[g][:].rearrange("p (c i) t -> p c t i", i=PACK), in_=q_raw[g][:].rearrange("p t (c i) -> p c t i", i=PACK))

        def quantise_q(g):
            nc.vector.quantize_mx(out=q_codes[g][:].bitcast(FP8X4), scales=q_scales[g][:], in_=q_bf[g][:].rearrange("p q t -> p (q t)"))

        def maxima(c):
            n0, width = CHUNKS[c]
            nc.vector.tensor_reduce(out=best[:, n0 // SEG:(n0 + width) // SEG], in_=acc[c][:].rearrange("p (j s) -> p j s", s=SEG),
                                    axis=mybir.AxisListType.X, op=mybir.AluOpType.max)

        for t in range(PACK):
            gather(0, t, 0, N)
            if t % 2:
                round_planes(nc.scalar.copy, 0, t - 1, t + 1, 0, N)
        gather(1, 0, 0, N)
        quantise_k(0, 0, N)
        for t in (1, 2):
            gather(1, t, 0, N)
            if t == 1:
                for n0, width in ((256, 256), (0, 256)):
                    round_planes(nc.scalar.copy, 1, 0, 2, n0, width)
        for n0, width in ((0, 384), (384, 128)):
            gather(1, 3, n0, width)
        round_q(nc.scalar.copy, 0)
        round_planes(nc.scalar.copy, 1, 2, 4, 0, 128)
        round_planes(nc.scalar.copy, 1, 2, 4, 288, 96)
        round_planes(nc.scalar.copy, 1, 2, 4, 384, 128)
        round_planes(nc.vector.tensor_copy, 1, 2, 4, 128, 160)
        quantise_q(0)
        q_bf.append(keep.tile([P, NQ, PACK], BF16, align_bytes=64, name="q_bf1", tag="q_raw0"))
        round_q(nc.vector.tensor_copy, 1)
        quantise_k(1, 0, 256)
        quantise_q(1)
        quantise_k(1, 256, STEP)
        quantise_k(1, 384, STEP)
        for g in range(PASSES):
            for c in range(4):
                multiply(g, c)
        for c in range(4):
            maxima(c)
        rows = out.rearrange("b q j -> (b q) j")
        nc.scalar.dma_start(out=rows[:, 0:16], in_=best[:, 0:16])
        nc.sync.dma_start(out=rows[:, 16:32], in_=best[:, 16:32])
